import numpy as np
import ml_dtypes

BF16 = ml_dtypes.bfloat16


def bf(x):
    return np.asarray(x, np.float32).astype(BF16)


def f32(x):
    return np.asarray(x, np.float32)


def f64(x):
    return np.asarray(x).astype(np.float64)


def striped(idx):
    return np.tile(idx.reshape(-1, 16).T, (8, 1))


S, K, M, N, B, Q = 512, 128, 128, 384, 2, 192


def setup_inputs():
    return {"base": bf(np.random.standard_normal((B, M, S))), "x": bf(np.random.standard_normal((K, N))), "w": bf(np.random.standard_normal((K, M)) / np.sqrt(K)), "offs": striped(np.random.permutation(S)[:N])}


def reference(base, x, w, offs):
    idx = offs[:16].T.reshape(-1)
    z = f64(base).copy()
    for i in range(B):
        z[i][:, idx[i * Q : (i + 1) * Q]] = f64(w).T @ f64(x)[:, i * Q : (i + 1) * Q]
    return z

@@ -1,0 +1,52 @@
+import concourse.mybir as mybir
+from concourse.masks import make_identity
+
+BF16, F32, U16 = mybir.dt.bfloat16, mybir.dt.float32, mybir.dt.uint16
+
+SEQS, FEATURES, TOKENS = 2, 128, 512
+CONTRACT, ENTRIES = 128, 384
+PIECE = ENTRIES // SEQS
+OFFSETS_A_COLUMN = 16
+PIECE_COLUMNS = PIECE // OFFSETS_A_COLUMN
+
+FLOPS = 2 * CONTRACT * FEATURES * ENTRIES
+
+
+def tile_scatter_matmul_kernel(tc, base, x, w, offs, out):
+    nc = tc.nc
+    with (
+        tc.tile_pool(name="held", bufs=1) as held,
+        tc.psum_pool(name="psum", bufs=1) as psum,
+    ):
+        base_tiles = [held.tile([FEATURES, TOKENS], BF16, name=f"base{i}") for i in range(SEQS)]
+        for i in range(SEQS):
+            nc.sync.dma_start(base_tiles[i][:], base[i])
+        weights = held.tile([CONTRACT, FEATURES], BF16)
+        nc.sync.dma_start(weights[:], w)
+        moving = held.tile([CONTRACT, ENTRIES], BF16)
+        nc.sync.dma_start(moving[:], x)
+        offsets = held.tile([128, ENTRIES // OFFSETS_A_COLUMN], U16)
+        nc.sync.dma_start(offsets[:], offs)
+
+        identity = held.tile([FEATURES, FEATURES], BF16)
+        make_identity(nc, identity[:])
+
+        windows = [psum.tile([FEATURES, TOKENS], F32, name=f"window{i}") for i in range(SEQS)]
+        for i in range(SEQS):
+            nc.tensor.matmul(windows[i][:], identity[:], base_tiles[i][:], start=True, stop=True)
+
+        for i in range(SEQS):
+            piece_offsets = offsets[:, i * PIECE_COLUMNS : (i + 1) * PIECE_COLUMNS]
+            nc.tensor.matmul(
+                windows[i][:].indirect(piece_offsets),
+                weights[:],
+                moving[:, i * PIECE : (i + 1) * PIECE],
+                start=True,
+                stop=True,
+            )
+
+        results = [held.tile([FEATURES, TOKENS], F32, name=f"result{i}") for i in range(SEQS)]
+        nc.vector.tensor_copy(results[0][:], windows[0][:])
+        nc.sync.dma_start(out[0], results[0][:])
+        nc.scalar.copy(results[1][:], windows[1][:])
+        nc.scalar.dma_start(out[1], results[1][:])

@@ -8,6 +8,7 @@ CONTRACT, ENTRIES = 128, 384
 PIECE = ENTRIES // SEQS
 OFFSETS_A_COLUMN = 16
 PIECE_COLUMNS = PIECE // OFFSETS_A_COLUMN
+WARM_UP_MATMULS = 4
 
 FLOPS = 2 * CONTRACT * FEATURES * ENTRIES
 
@@ -27,6 +28,12 @@ def tile_scatter_matmul_kernel(tc, base, x, w, offs, out):
         nc.sync.dma_start(moving[:], x)
         offsets = held.tile([128, ENTRIES // OFFSETS_A_COLUMN], U16)
         nc.sync.dma_start(offsets[:], offs)
+
+        zeros = held.tile([CONTRACT, TOKENS], BF16)
+        nc.vector.memset(zeros[:], 0.0)
+        spare = psum.tile([FEATURES, TOKENS], F32)
+        for warm_up in range(WARM_UP_MATMULS):
+            nc.tensor.matmul(spare[:], zeros[:, :FEATURES], zeros[:], start=True, stop=True)
 
         identity = held.tile([FEATURES, FEATURES], BF16)
         make_identity(nc, identity[:])

@@ -8,7 +8,7 @@ CONTRACT, ENTRIES = 128, 384
 PIECE = ENTRIES // SEQS
 OFFSETS_A_COLUMN = 16
 PIECE_COLUMNS = PIECE // OFFSETS_A_COLUMN
-WARM_UP_MATMULS = 4
+WARM_UP_MATMULS = 2
 
 FLOPS = 2 * CONTRACT * FEATURES * ENTRIES
 
@@ -30,7 +30,7 @@ def tile_scatter_matmul_kernel(tc, base, x, w, offs, out):
         nc.sync.dma_start(offsets[:], offs)
 
         zeros = held.tile([CONTRACT, TOKENS], BF16)
-        nc.vector.memset(zeros[:], 0.0)
+        nc.gpsimd.memset(zeros[:], 0.0)
         spare = psum.tile([FEATURES, TOKENS], F32)
         for warm_up in range(WARM_UP_MATMULS):
             nc.tensor.matmul(spare[:], zeros[:, :FEATURES], zeros[:], start=True, stop=True)

import concourse.mybir as mybir
from concourse.masks import make_identity

BF16, F32, U16 = mybir.dt.bfloat16, mybir.dt.float32, mybir.dt.uint16

SEQS, FEATURES, TOKENS = 2, 128, 512
CONTRACT, ENTRIES = 128, 384
PIECE = ENTRIES // SEQS
OFFSETS_A_COLUMN = 16
PIECE_COLUMNS = PIECE // OFFSETS_A_COLUMN
WARM_UP_MATMULS = 2

FLOPS = 2 * CONTRACT * FEATURES * ENTRIES


def tile_scatter_matmul_kernel(tc, base, x, w, offs, out):
    nc = tc.nc
    with (
        tc.tile_pool(name="held", bufs=1) as held,
        tc.psum_pool(name="psum", bufs=1) as psum,
    ):
        base_tiles = [held.tile([FEATURES, TOKENS], BF16, name=f"base{i}") for i in range(SEQS)]
        for i in range(SEQS):
            nc.sync.dma_start(base_tiles[i][:], base[i])
        weights = held.tile([CONTRACT, FEATURES], BF16)
        nc.sync.dma_start(weights[:], w)
        moving = held.tile([CONTRACT, ENTRIES], BF16)
        nc.sync.dma_start(moving[:], x)
        offsets = held.tile([128, ENTRIES // OFFSETS_A_COLUMN], U16)
        nc.sync.dma_start(offsets[:], offs)

        zeros = held.tile([CONTRACT, TOKENS], BF16)
        nc.gpsimd.memset(zeros[:], 0.0)
        spare = psum.tile([FEATURES, TOKENS], F32)
        for warm_up in range(WARM_UP_MATMULS):
            nc.tensor.matmul(spare[:], zeros[:, :FEATURES], zeros[:], start=True, stop=True)

        identity = held.tile([FEATURES, FEATURES], BF16)
        make_identity(nc, identity[:])

        windows = [psum.tile([FEATURES, TOKENS], F32, name=f"window{i}") for i in range(SEQS)]
        for i in range(SEQS):
            nc.tensor.matmul(windows[i][:], identity[:], base_tiles[i][:], start=True, stop=True)

        for i in range(SEQS):
            piece_offsets = offsets[:, i * PIECE_COLUMNS : (i + 1) * PIECE_COLUMNS]
            nc.tensor.matmul(
                windows[i][:].indirect(piece_offsets),
                weights[:],
                moving[:, i * PIECE : (i + 1) * PIECE],
                start=True,
                stop=True,
            )

        results = [held.tile([FEATURES, TOKENS], F32, name=f"result{i}") for i in range(SEQS)]
        nc.vector.tensor_copy(results[0][:], windows[0][:])
        nc.sync.dma_start(out[0], results[0][:])
        nc.scalar.copy(results[1][:], windows[1][:])
        nc.scalar.dma_start(out[1], results[1][:])
